import numpy as np, ml_dtypes
CORES = [2,6,26,30,66,70,74,78,82,86]
N = 10
WB, KB, QP = 1, 1, 32
def setup_inputs(rng):
    return {"q": rng.standard_normal((N, 128, QP), dtype=np.float32).astype(ml_dtypes.bfloat16), "k": rng.standard_normal((N, 128, KB * 128), dtype=np.float32).astype(ml_dtypes.bfloat16), "v": rng.standard_normal((N, 128, KB * 128), dtype=np.float32).astype(ml_dtypes.bfloat16)}
def setup_inputs_big(rng):
    d = setup_inputs(rng)
    for k in ("q", "k", "v"): d[k] = (d[k].astype(np.float32) * 1024.0).astype(d[k].dtype)
    return d
def setup_inputs_small(rng):
    d = setup_inputs(rng)
    for k in ("q", "k", "v"): d[k] = (d[k].astype(np.float32) * (1 / 1024.0)).astype(d[k].dtype)
    return d
def setup_inputs_apart(rng):
    d = setup_inputs(rng)
    f = (10.0 ** rng.permutation(np.linspace(-1.5, 1.5, N))).astype(np.float32).reshape(N, 1, 1)
    for k in ("q", "k", "v"): d[k] = (d[k].astype(np.float32) * f).astype(d[k].dtype)
    return d
def reference(q, k, v):
    Q, K, V = q.astype(np.float64), k.astype(np.float64), v.astype(np.float64)
    y = np.zeros((N, 128, QP))
    for r in range(N):
        for j in range(max(0, r - WB), r + 1):
            for b in range(KB):
                S = np.maximum(K[j][:, 128 * b:128 * b + 128].T @ Q[r], 0.0)
                y[r] += V[j][:, 128 * b:128 * b + 128].T @ S
    return {"y": y.astype(ml_dtypes.bfloat16 if q.dtype != np.float64 else np.float64)}

@@ -1,0 +1,79 @@
+SCRATCH = {
+    "kv": ("sbuf", [128, 256], "bfloat16"),
+    "kvp": ("sbuf", [128, 256], "bfloat16"),
+    "qs": ("sbuf", [128, 32], "bfloat16"),
+    "zero": ("sbuf", [128, 32], "float32"),
+    "p0": ("sbuf", [128, 32], "bfloat16"),
+    "p1": ("sbuf", [128, 32], "bfloat16"),
+    "ys": ("sbuf", [128, 32], "bfloat16"),
+    "s0": ("psum", [128, 512], "float32"),
+    "s1": ("psum", [128, 512], "float32"),
+    "o": ("psum", [128, 512], "float32"),
+}
+SEMAPHORES = ["ldkv", "ldq", "zs", "arr", "sent", "m0", "r0", "m1", "r1", "m2", "cp", "st"]
+
+from concourse.mybir import AluOpType
+
+ENGINES = 8
+
+
+def _engines(mask, want):
+    out, n, bit = 0, 0, 1
+    while bit <= mask and n < want:
+        if mask & bit:
+            out |= bit
+            n += 1
+        bit <<= 1
+    return out, n
+
+
+def rank_program(g, core, T, topo):
+    rank = T.rank_of(core)
+    if rank is None:
+        return
+    cores = T.cores
+    last = len(cores) - 1
+    S = T.sem
+    k, v = T.kv[:, 0:128], T.kv[:, 128:256]
+    kp, vp = T.kvp[:, 0:128], T.kvp[:, 128:256]
+    s0, s1, o = T.s0[:, 0:32], T.s1[:, 0:32], T.o[:, 0:32]
+
+    g.sync.dma_start(k, T.k[:]).then_inc(S.ldkv, 16)
+    g.scalar.dma_start(v, T.v[:]).then_inc(S.ldkv, 16)
+    g.sync.dma_start(T.qs[:], T.q[:]).then_inc(S.ldq, 16)
+    g.vector.memset(T.zero[:], 0.0).then_inc(S.zs, 1)
+
+    if rank < last:
+        dst = cores[rank + 1]
+        assert topo.may_write(core, dst)
+        rid, pid, _ = topo.addr(dst)
+        mask, n_out = _engines(topo.mask(core, dst), ENGINES)
+        g.wait_ge(S.ldkv, 32)
+        g.remote_dma(T.kvp[:], T.kv[:], S.arr, S.sent, pid, rid, mask)
+
+    g.tensor.wait_ge(S.ldkv, 32)
+    g.tensor.wait_ge(S.ldq, 16)
+    g.tensor.matmul(s0, k, T.qs[:], start=True, stop=True).then_inc(S.m0, 1)
+    g.vector.wait_ge(S.zs, 1)
+    g.vector.wait_ge(S.m0, 1)
+    g.vector.tensor_tensor(T.p0[:], s0, T.zero[:], AluOpType.max).then_inc(S.r0, 1)
+    g.tensor.wait_ge(S.r0, 1)
+    if rank == 0:
+        g.tensor.matmul(o, v, T.p0[:], start=True, stop=True).then_inc(S.m2, 1)
+    else:
+        g.tensor.matmul(o, v, T.p0[:], start=True, stop=False)
+        _, n_in = _engines(topo.mask(cores[rank - 1], core), ENGINES)
+        g.tensor.wait_ge(S.arr, n_in)
+        g.tensor.matmul(s1, kp, T.qs[:], start=True, stop=True).then_inc(S.m1, 1)
+        g.vector.wait_ge(S.m1, 1)
+        g.vector.tensor_tensor(T.p1[:], s1, T.zero[:], AluOpType.max).then_inc(S.r1, 1)
+        g.tensor.wait_ge(S.r1, 1)
+        g.tensor.matmul(o, vp, T.p1[:], start=False, stop=True).then_inc(S.m2, 1)
+
+    g.vector.wait_ge(S.m2, 1)
+    g.vector.tensor_copy(T.ys[:], o).then_inc(S.cp, 1)
+    g.sync.wait_ge(S.cp, 1)
+    g.sync.dma_start(T.y[:], T.ys[:]).then_inc(S.st, 16)
+    g.sync.wait_ge(S.st, 16)
+    if rank < last:
+        g.wait_ge(S.sent, n_out)

@@ -1,16 +1,24 @@
+G = 2
+M = 128 // G
+W = 32 * G
+
 SCRATCH = {
-    "kv": ("sbuf", [128, 256], "bfloat16"),
-    "kvp": ("sbuf", [128, 256], "bfloat16"),
+    "ks": ("sbuf", [128, 128], "bfloat16"),
+    "vs": ("sbuf", [128, 128], "bfloat16"),
+    "kp": ("sbuf", [128, 128], "bfloat16"),
+    "vp": ("sbuf", [128, 128], "bfloat16"),
     "qs": ("sbuf", [128, 32], "bfloat16"),
     "zero": ("sbuf", [128, 32], "float32"),
     "p0": ("sbuf", [128, 32], "bfloat16"),
     "p1": ("sbuf", [128, 32], "bfloat16"),
-    "ys": ("sbuf", [128, 32], "bfloat16"),
+    "own": ("sbuf", [128, W], "float32"),
+    "ys": ("sbuf", [128, W], "bfloat16"),
     "s0": ("psum", [128, 512], "float32"),
     "s1": ("psum", [128, 512], "float32"),
-    "o": ("psum", [128, 512], "float32"),
+    "o0": ("psum", [128, 512], "float32"),
+    "o1": ("psum", [128, 512], "float32"),
 }
-SEMAPHORES = ["ldkv", "ldq", "zs", "arr", "sent", "m0", "r0", "m1", "r1", "m2", "cp", "st"]
+SEMAPHORES = ["ldk", "ldv", "ldq", "zs", "arrk", "arrv", "sent", "m0", "r0", "n0", "c0", "m1", "r1", "n1", "cp", "st"]
 
 from concourse.mybir import AluOpType
 
@@ -34,12 +42,11 @@ def rank_program(g, core, T, topo):
     cores = T.cores
     last = len(cores) - 1
     S = T.sem
-    k, v = T.kv[:, 0:128], T.kv[:, 128:256]
-    kp, vp = T.kvp[:, 0:128], T.kvp[:, 128:256]
-    s0, s1, o = T.s0[:, 0:32], T.s1[:, 0:32], T.o[:, 0:32]
+    s0, s1 = T.s0[:, 0:32], T.s1[:, 0:32]
+    ys = T.ys[0:M, :]
 
-    g.sync.dma_start(k, T.k[:]).then_inc(S.ldkv, 16)
-    g.scalar.dma_start(v, T.v[:]).then_inc(S.ldkv, 16)
+    g.sync.dma_start(T.ks[:], T.k[:]).then_inc(S.ldk, 16)
+    g.scalar.dma_start(T.vs[:], T.v[:]).then_inc(S.ldv, 16)
     g.sync.dma_start(T.qs[:], T.q[:]).then_inc(S.ldq, 16)
     g.vector.memset(T.zero[:], 0.0).then_inc(S.zs, 1)
 
@@ -48,32 +55,43 @@ def rank_program(g, core, T, topo):
         assert topo.may_write(core, dst)
         rid, pid, _ = topo.addr(dst)
         mask, n_out = _engines(topo.mask(core, dst), ENGINES)
-        g.wait_ge(S.ldkv, 32)
-        g.remote_dma(T.kvp[:], T.kv[:], S.arr, S.sent, pid, rid, mask)
+        g.wait_ge(S.ldk, 16)
+        g.remote_dma(T.kp[:], T.ks[:], S.arrk, S.sent, pid, rid, mask)
+        g.wait_ge(S.ldv, 16)
+        g.remote_dma(T.vp[:], T.vs[:], S.arrv, S.sent, pid, rid, mask)
 
-    g.tensor.wait_ge(S.ldkv, 32)
+    def times_v(out, buf, p, sem):
+        for a in range(G):
+            g.tensor.matmul(out[0:M, 32 * a:32 * a + 32], buf[:, a:128:G], p, start=True, stop=True).then_inc(sem, 1)
+
+    g.tensor.wait_ge(S.ldk, 16)
     g.tensor.wait_ge(S.ldq, 16)
-    g.tensor.matmul(s0, k, T.qs[:], start=True, stop=True).then_inc(S.m0, 1)
+    g.tensor.matmul(s0, T.ks[:], T.qs[:], start=True, stop=True).then_inc(S.m0, 1)
     g.vector.wait_ge(S.zs, 1)
     g.vector.wait_ge(S.m0, 1)
     g.vector.tensor_tensor(T.p0[:], s0, T.zero[:], AluOpType.max).then_inc(S.r0, 1)
     g.tensor.wait_ge(S.r0, 1)
+    g.tensor.wait_ge(S.ldv, 16)
+    times_v(T.o0, T.vs, T.p0[:], S.n0)
+    g.vector.wait_ge(S.n0, G)
     if rank == 0:
-        g.tensor.matmul(o, v, T.p0[:], start=True, stop=True).then_inc(S.m2, 1)
+        g.vector.tensor_copy(ys, T.o0[0:M, 0:W]).then_inc(S.cp, 1)
     else:
-        g.tensor.matmul(o, v, T.p0[:], start=True, stop=False)
+        g.vector.tensor_copy(T.own[0:M, :], T.o0[0:M, 0:W]).then_inc(S.c0, 1)
         _, n_in = _engines(topo.mask(cores[rank - 1], core), ENGINES)
-        g.tensor.wait_ge(S.arr, n_in)
-        g.tensor.matmul(s1, kp, T.qs[:], start=True, stop=True).then_inc(S.m1, 1)
+        g.tensor.wait_ge(S.arrk, n_in)
+        g.tensor.matmul(s1, T.kp[:], T.qs[:], start=True, stop=True).then_inc(S.m1, 1)
+        g.vector.wait_ge(S.c0, 1)
         g.vector.wait_ge(S.m1, 1)
         g.vector.tensor_tensor(T.p1[:], s1, T.zero[:], AluOpType.max).then_inc(S.r1, 1)
         g.tensor.wait_ge(S.r1, 1)
-        g.tensor.matmul(o, vp, T.p1[:], start=False, stop=True).then_inc(S.m2, 1)
+        g.tensor.wait_ge(S.arrv, n_in)
+        times_v(T.o1, T.vp, T.p1[:], S.n1)
+        g.vector.wait_ge(S.n1, G)
+        g.vector.tensor_tensor(ys, T.o1[0:M, 0:W], T.own[0:M, :], AluOpType.add).then_inc(S.cp, 1)
 
-    g.vector.wait_ge(S.m2, 1)
-    g.vector.tensor_copy(T.ys[:], o).then_inc(S.cp, 1)
     g.sync.wait_ge(S.cp, 1)
-    g.sync.dma_start(T.y[:], T.ys[:]).then_inc(S.st, 16)
+    g.sync.dma_start(T.y[:], ys).then_inc(S.st, 16)
     g.sync.wait_ge(S.st, 16)
     if rank < last:
-        g.wait_ge(S.sent, n_out)
+        g.wait_ge(S.sent, 2 * n_out)

G = 2
M = 128 // G
W = 32 * G

SCRATCH = {
    "ks": ("sbuf", [128, 128], "bfloat16"),
    "vs": ("sbuf", [128, 128], "bfloat16"),
    "kp": ("sbuf", [128, 128], "bfloat16"),
    "vp": ("sbuf", [128, 128], "bfloat16"),
    "qs": ("sbuf", [128, 32], "bfloat16"),
    "zero": ("sbuf", [128, 32], "float32"),
    "p0": ("sbuf", [128, 32], "bfloat16"),
    "p1": ("sbuf", [128, 32], "bfloat16"),
    "own": ("sbuf", [128, W], "float32"),
    "ys": ("sbuf", [128, W], "bfloat16"),
    "s0": ("psum", [128, 512], "float32"),
    "s1": ("psum", [128, 512], "float32"),
    "o0": ("psum", [128, 512], "float32"),
    "o1": ("psum", [128, 512], "float32"),
}
SEMAPHORES = ["ldk", "ldv", "ldq", "zs", "arrk", "arrv", "sent", "m0", "r0", "n0", "c0", "m1", "r1", "n1", "cp", "st"]

from concourse.mybir import AluOpType

ENGINES = 8


def _engines(mask, want):
    out, n, bit = 0, 0, 1
    while bit <= mask and n < want:
        if mask & bit:
            out |= bit
            n += 1
        bit <<= 1
    return out, n


def rank_program(g, core, T, topo):
    rank = T.rank_of(core)
    if rank is None:
        return
    cores = T.cores
    last = len(cores) - 1
    S = T.sem
    s0, s1 = T.s0[:, 0:32], T.s1[:, 0:32]
    ys = T.ys[0:M, :]

    g.sync.dma_start(T.ks[:], T.k[:]).then_inc(S.ldk, 16)
    g.scalar.dma_start(T.vs[:], T.v[:]).then_inc(S.ldv, 16)
    g.sync.dma_start(T.qs[:], T.q[:]).then_inc(S.ldq, 16)
    g.vector.memset(T.zero[:], 0.0).then_inc(S.zs, 1)

    if rank < last:
        dst = cores[rank + 1]
        assert topo.may_write(core, dst)
        rid, pid, _ = topo.addr(dst)
        mask, n_out = _engines(topo.mask(core, dst), ENGINES)
        g.wait_ge(S.ldk, 16)
        g.remote_dma(T.kp[:], T.ks[:], S.arrk, S.sent, pid, rid, mask)
        g.wait_ge(S.ldv, 16)
        g.remote_dma(T.vp[:], T.vs[:], S.arrv, S.sent, pid, rid, mask)

    def times_v(out, buf, p, sem):
        for a in range(G):
            g.tensor.matmul(out[0:M, 32 * a:32 * a + 32], buf[:, a:128:G], p, start=True, stop=True).then_inc(sem, 1)

    g.tensor.wait_ge(S.ldk, 16)
    g.tensor.wait_ge(S.ldq, 16)
    g.tensor.matmul(s0, T.ks[:], T.qs[:], start=True, stop=True).then_inc(S.m0, 1)
    g.vector.wait_ge(S.zs, 1)
    g.vector.wait_ge(S.m0, 1)
    g.vector.tensor_tensor(T.p0[:], s0, T.zero[:], AluOpType.max).then_inc(S.r0, 1)
    g.tensor.wait_ge(S.r0, 1)
    g.tensor.wait_ge(S.ldv, 16)
    times_v(T.o0, T.vs, T.p0[:], S.n0)
    g.vector.wait_ge(S.n0, G)
    if rank == 0:
        g.vector.tensor_copy(ys, T.o0[0:M, 0:W]).then_inc(S.cp, 1)
    else:
        g.vector.tensor_copy(T.own[0:M, :], T.o0[0:M, 0:W]).then_inc(S.c0, 1)
        _, n_in = _engines(topo.mask(cores[rank - 1], core), ENGINES)
        g.tensor.wait_ge(S.arrk, n_in)
        g.tensor.matmul(s1, T.kp[:], T.qs[:], start=True, stop=True).then_inc(S.m1, 1)
        g.vector.wait_ge(S.c0, 1)
        g.vector.wait_ge(S.m1, 1)
        g.vector.tensor_tensor(T.p1[:], s1, T.zero[:], AluOpType.max).then_inc(S.r1, 1)
        g.tensor.wait_ge(S.r1, 1)
        g.tensor.wait_ge(S.arrv, n_in)
        times_v(T.o1, T.vp, T.p1[:], S.n1)
        g.vector.wait_ge(S.n1, G)
        g.vector.tensor_tensor(ys, T.o1[0:M, 0:W], T.own[0:M, :], AluOpType.add).then_inc(S.cp, 1)

    g.sync.wait_ge(S.cp, 1)
    g.sync.dma_start(T.y[:], ys).then_inc(S.st, 16)
    g.sync.wait_ge(S.st, 16)
    if rank < last:
        g.wait_ge(S.sent, 2 * n_out)
